import numpy as np
import ml_dtypes


def mxq(x, axis, fmt="e4m3"):
    dtype, down = {"e4m3": (ml_dtypes.float8_e4m3fn, 7), "e5m2": (ml_dtypes.float8_e5m2, 14)}[fmt]
    v = np.moveaxis(np.asarray(x, np.float32).astype(ml_dtypes.bfloat16).astype(np.float64), axis, -1)
    blocks = v.reshape(v.shape[:-1] + (-1, 32))
    amax = np.abs(blocks).max(-1, keepdims=True)
    byte = np.maximum(np.where(amax > 0, np.frexp(amax)[1] - 1 + 127, 0) - down, 1)
    scale = np.exp2(byte - 127.0)
    codes = (blocks / scale).astype(np.float32).astype(dtype).astype(np.float64)
    return np.moveaxis((codes * scale).reshape(v.shape), -1, axis)


WIDE = False


def mx_kscale(k):
    if not WIDE:
        return np.ones(k)
    levels = np.array([10, -10, 5, -5, 0])
    if k % 512:
        return np.exp2(np.random.permutation(np.resize(levels, k // 32))).repeat(32)
    a = np.empty((k // 512, 16))
    for p in range(k // 512):
        a[p, :8] = np.random.permutation(np.resize(levels, 8))
        for g in range(8):
            far = levels[np.abs(levels - a[p, g]) >= 10]
            a[p, g + 8] = far[np.random.randint(len(far))]
    return np.exp2(a.ravel()).repeat(32)


BF16 = ml_dtypes.bfloat16


def bf(x):
    return np.asarray(x, np.float32).astype(BF16)


def f64(x):
    return np.asarray(x).astype(np.float64)


E2M1 = np.array([0.0, 0.5, 1.0, 1.5, 2.0, 3.0, 4.0, 6.0, -0.0, -0.5, -1.0, -1.5, -2.0, -3.0, -4.0, -6.0])


def pack_weight(w, fmt):
    k, n = w.shape
    w = f64(bf(w)).reshape(k // 32, 32, n)
    amax = np.abs(w).max(1)
    if fmt == "e4m3":
        byte = np.frexp(amax)[1] - 1 + 127 - 7
    else:
        mant, ex = np.frexp(amax / 6.0)
        byte = np.where(mant > 0.5, ex, ex - 1) + 127
    byte = np.clip(np.where(amax > 0, byte, 1), 1, 254)
    scaled = (w * np.exp2(127.0 - byte)[:, None, :]).reshape(k, n).astype(np.float32)
    by_word = np.ascontiguousarray(scaled.reshape(k // 512, 128, 4, n).transpose(0, 1, 3, 2))
    if fmt == "e4m3":
        words = by_word.astype(ml_dtypes.float8_e4m3fn).view(np.uint8)
    else:
        c = by_word.astype(ml_dtypes.float4_e2m1fn).view(np.uint8) & 0xF
        words = c[..., 0::2] | (c[..., 1::2] << 4)
    return np.ascontiguousarray(words), np.ascontiguousarray(byte.astype(np.uint8).reshape(k // 512, 16, n))


def unpack_weight(words, scales, fmt):
    g, p, n, _ = words.shape
    if fmt == "e4m3":
        vals = np.ascontiguousarray(words).view(ml_dtypes.float8_e4m3fn).astype(np.float64)
    else:
        nib = np.empty((g, p, n, 4), np.uint8)
        nib[..., 0::2] = words & 0xF
        nib[..., 1::2] = words >> 4
        vals = E2M1[nib]
    vals = vals * np.repeat(np.exp2(scales.astype(np.float64) - 127.0), 8, axis=1)[..., None]
    return vals.transpose(0, 1, 3, 2).reshape(g * 512, n)
def pack4(w):
    words, scales = pack_weight(w, "e2m1")
    return words.reshape(words.shape[0], 128, -1), scales


def unpack4(words, scales):
    return unpack_weight(words.reshape(words.shape[0], 128, -1, 2), scales, "e2m1")


M, K, N = 1024, 2048, 512


def setup_inputs():
    s = mx_kscale(K)
    chosen = np.random.standard_normal((M, K)) * s
    rejected = np.random.standard_normal((M, K)) * s
    base = np.random.standard_normal((K, N)) / np.sqrt(2 * K) / s[:, None]
    salience = np.random.standard_normal((K, N)) / np.sqrt(2 * K) / s[:, None]
    tuned = 0.7 * np.random.standard_normal((K, N)) / np.sqrt(2 * K) / s[:, None]
    base_words, base_scales = pack4(base)
    salience_words, salience_scales = pack_weight(salience, "e4m3")
    return {"chosen": bf(chosen),
            "rejected": bf(rejected),
            "base_words": base_words,
            "base_scales": base_scales,
            "salience_words": salience_words,
            "salience_scales": salience_scales,
            "tuned": bf(tuned),
            "strength": bf(1 + 0.1 * np.random.standard_normal(N))}


def reference(chosen, rejected, base_words, base_scales, salience_words, salience_scales, tuned, strength):
    d = mxq(f64(chosen) - f64(rejected), 1, "e4m3")
    a = d @ unpack4(base_words, base_scales)
    v = d @ unpack_weight(salience_words, salience_scales, "e4m3")
    r = d @ mxq(f64(tuned), 0, "e4m3")
    return (a + r) * np.abs(v) * f64(strength)

@@ -1,0 +1,326 @@
+from contextlib import ExitStack
+
+import concourse.mybir as mybir
+from concourse.masks import make_identity
+
+M, K, N = 1024, 2048, 512
+FLOPS = 3 * 2 * M * K * N
+
+F32 = mybir.dt.float32
+BF16 = mybir.dt.bfloat16
+U32 = mybir.dt.uint32
+I32 = mybir.dt.int32
+U8 = mybir.dt.uint8
+FP8X4 = mybir.dt.float8_e4m3fn_x4
+FP4X4 = mybir.dt.float4_e2m1fn_x4
+ALU = mybir.AluOpType
+ACT = mybir.ActivationFunctionType
+
+P = 128
+PASSES = K // 512
+TILES = M // P
+HALF = K // 2
+SPLIT = 3
+FACTORS = 8
+V_BANKS = [2, 3, 4, 2, 2, 2, 2, 2]
+AR_BANKS = [5, 6, 7, 3, 4, 5, 6, 7]
+VCOLS = 256
+RING = 4
+
+
+def tile_preference_attribute_margins_s10_kernel(
+    tc, chosen, rejected, base_words, base_scales, salience_words, salience_scales, tuned, strength, out
+):
+    nc = tc.nc
+    with ExitStack() as ctx:
+        sb = ctx.enter_context(tc.tile_pool(name="sb", bufs=1))
+        ps = ctx.enter_context(tc.psum_pool(name="ps", bufs=1))
+        ctx.enter_context(tc.manual_schedule())
+
+        def tiles(pool, stem, count, shape, dtype):
+            return [pool.tile(shape, dtype, name="%s%d" % (stem, j), align_bytes=64) for j in range(count)]
+
+        bank = [ps.tile([P, N], F32, name="bank%d" % j) for j in range(8)]
+        turn_bank = bank[:2]
+        v_bank = [bank[j] for j in V_BANKS]
+        ar_bank = [bank[j] for j in AR_BANKS]
+
+        ident = sb.tile([P, P], F32, name="ident", align_bytes=64)
+        c_half = tiles(sb, "ch", 2 * SPLIT, [P, HALF], BF16)
+        r_half = tiles(sb, "rh", 2 * SPLIT, [P, HALF], BF16)
+        c_raw = tiles(sb, "c", TILES - SPLIT, [P, K], BF16)
+        r_raw = tiles(sb, "r", TILES - SPLIT, [P, K], BF16)
+        sal_codes = tiles(sb, "sc", 2, [P, 2, N], U32)
+        sal_plane = sb.tile([P, N], U8, name="sp", align_bytes=64)
+        base_codes = tiles(sb, "bc", 2, [P, 2, 2 * N], U8)
+        base_plane = sb.tile([P, PASSES, N], U8, name="bp", align_bytes=64)
+        tuned_raw = tiles(sb, "tr", PASSES, [P, 4, N], BF16)
+        tuned_mix = tiles(sb, "tm", PASSES, [P, 4 * N], BF16)
+        tuned_codes = tiles(sb, "tc", PASSES, [P, N], U32)
+        tuned_plane = tiles(sb, "tp", PASSES, [P, N], U8)
+        d_sorted = tiles(sb, "d", RING, [P, HALF], BF16)
+        d_turned = tiles(sb, "dt", RING, [P, HALF], BF16)
+        d_codes = tiles(sb, "dc", 2 * TILES, [P, 2 * P], U32)
+        d_plane = tiles(sb, "dp", 2 * TILES, [P, 2 * P], U8)
+        factor = tiles(sb, "w", FACTORS, [P, N], F32)
+        result = tiles(sb, "o", TILES, [P, N], F32)
+        gain_raw = sb.tile([P, 4], BF16, name="gr", align_bytes=64)
+        gain_col = sb.tile([P, 4], F32, name="gc", align_bytes=64)
+        gain = sb.tile([P, N], F32, name="gain", align_bytes=64)
+        table_in = sb.tile([P, 1], F32, name="ti", align_bytes=64)
+        table_out = sb.tile([P, 1], F32, name="to", align_bytes=64)
+
+        def slot(i, h):
+            return (h * SPLIT + i if i < SPLIT else 2 * i + h) % RING
+
+        def rows(i):
+            return slice(i * P, (i + 1) * P)
+
+        def load_pair(i):
+            nc.sync.dma_start(out=c_raw[i - SPLIT][:], in_=chosen[rows(i), :])
+            nc.sync.dma_start(out=r_raw[i - SPLIT][:], in_=rejected[rows(i), :])
+
+        def load_half(i, h):
+            cols = slice(h * HALF, (h + 1) * HALF)
+            nc.sync.dma_start(out=c_half[2 * i + h][:], in_=chosen[rows(i), cols])
+            nc.sync.dma_start(out=r_half[2 * i + h][:], in_=rejected[rows(i), cols])
+
+        def load_salience(h):
+            src = salience_words[2 * h : 2 * h + 2].rearrange("g p n t -> p g (n t)").bitcast(I32)
+            nc.sync.dma_start(out=sal_codes[h][:].bitcast(I32), in_=src)
+
+        def load_base(h):
+            src = base_words[2 * h : 2 * h + 2].rearrange("g p b -> p g b").bitcast(I32)
+            nc.sync.dma_start(out=base_codes[h][:].bitcast(I32), in_=src)
+
+        def load_sal_scales(eng):
+            for q in range(4):
+                src = salience_scales[:, 4 * q : 4 * q + 4, :].bitcast(I32)
+                eng.dma_start(out=sal_plane[32 * q : 32 * q + 16, :].bitcast(I32), in_=src)
+
+        def load_base_scales(eng):
+            for q in range(4):
+                src = base_scales[:, 4 * q : 4 * q + 4, :].rearrange("g r n -> r g n").bitcast(I32)
+                eng.dma_start(out=base_plane[32 * q : 32 * q + 4, :, :].bitcast(I32), in_=src)
+
+        def load_tuned(g):
+            src = tuned[g * 512 : (g + 1) * 512, :].rearrange("(p t) n -> p t n", t=4)
+            nc.sync.dma_start(out=tuned_raw[g][:], in_=src)
+
+        def subtract(i, h):
+            cols = slice(h * HALF, (h + 1) * HALF)
+            a = c_half[2 * i + h][:] if i < SPLIT else c_raw[i - SPLIT][:, cols]
+            b = r_half[2 * i + h][:] if i < SPLIT else r_raw[i - SPLIT][:, cols]
+            nc.vector.tensor_tensor(
+                out=d_sorted[slot(i, h)][:].rearrange("p (u w e) -> p u w e", u=2, e=2),
+                in0=a.rearrange("p (w u e) -> p u w e", u=2, e=2),
+                in1=b.rearrange("p (w u e) -> p u w e", u=2, e=2),
+                op=ALU.subtract,
+            )
+
+        def turn(i, h, b):
+            words = d_sorted[slot(i, h)][:].bitcast(F32)
+            for g in range(2):
+                for u in range(2):
+                    j = 2 * g + u
+                    s = u * 2 * P + g * P
+                    nc.tensor.transpose(turn_bank[b][:, j * P : (j + 1) * P], words[:, s : s + P], ident[:])
+
+        def evacuate(i, h, b):
+            nc.scalar.copy(
+                out=d_turned[slot(i, h)][:].bitcast(F32).rearrange("p (g m u) -> p g m u", g=2, u=2),
+                in_=turn_bank[b][:].rearrange("p (g u m) -> p g m u", g=2, u=2),
+            )
+
+        def quantize_d(i, h):
+            nc.vector.quantize_mx(
+                out=d_codes[2 * i + h][:].bitcast(FP8X4), scales=d_plane[2 * i + h][:], in_=d_turned[slot(i, h)][:]
+            )
+
+        def mx(bank, i, g, rhs, rhs_scale, start, stop):
+            cols = slice((g % 2) * P, (g % 2 + 1) * P)
+            nc.tensor.matmul_mx(
+                out=bank[:],
+                lhsT=d_codes[2 * i + g // 2][:, cols].bitcast(FP8X4),
+                lhsT_scale=d_plane[2 * i + g // 2][:, cols],
+                rhs=rhs,
+                rhs_scale=rhs_scale,
+                start=start,
+                stop=stop,
+            )
+
+        def mul_v(i, passes=range(PASSES)):
+            for g in passes:
+                mx(v_bank[i], i, g, sal_codes[g // 2][:, g % 2, :].bitcast(FP8X4), sal_plane[4 * g :, :], g == 0, g == PASSES - 1)
+
+        def mul_a(i, passes=range(PASSES)):
+            for g in passes:
+                mx(ar_bank[i], i, g, base_codes[g // 2][:, g % 2, :].bitcast(FP4X4), base_plane[:, g, :], g == 0, False)
+
+        def mul_r(i, g):
+            mx(ar_bank[i], i, g, tuned_codes[g][:].bitcast(FP8X4), tuned_plane[g][:], False, g == PASSES - 1)
+
+        def mix(copy, g, c0, c1):
+            copy(
+                out=tuned_mix[g][:, 4 * c0 : 4 * c1].rearrange("p (c i t) -> p c t i", i=4, t=4),
+                in_=tuned_raw[g][:, :, c0:c1].rearrange("p t (c i) -> p c t i", i=4),
+            )
+
+        def mix_vector(g):
+            mix(nc.vector.tensor_copy, g, 0, VCOLS)
+
+        def mix_scalar(g):
+            mix(nc.scalar.copy, g, VCOLS, N)
+
+        def quantize_tuned(g):
+            nc.vector.quantize_mx(out=tuned_codes[g][:].bitcast(FP8X4), scales=tuned_plane[g][:], in_=tuned_mix[g][:])
+
+        def take_abs(i):
+            nc.scalar.activation(out=factor[i % FACTORS][:], in_=v_bank[i][:], func=ACT.Abs)
+
+        def weigh(i):
+            nc.vector.tensor_tensor(out=factor[i % FACTORS][:], in0=factor[i % FACTORS][:], in1=gain[:], op=ALU.mult)
+
+        def finish(i):
+            nc.vector.tensor_tensor(out=result[i][:], in0=ar_bank[i][:], in1=factor[i % FACTORS][:], op=ALU.mult)
+
+        def store(i):
+            nc.sync.dma_start(out=out[rows(i), :], in_=result[i][:])
+
+        def spread_gain(b):
+            nc.vector.tensor_copy(out=gain_col[:], in_=gain_raw[:])
+            for c in range(4):
+                nc.tensor.transpose(b[:, c * P : (c + 1) * P], gain_col[:, c : c + 1].to_broadcast([P, P]), ident[:])
+            nc.scalar.copy(out=gain[:].rearrange("p (q c) -> p q c", c=4), in_=b[:].rearrange("p (c q) -> p q c", c=4))
+
+        def load_gain():
+            nc.sync.dma_start(out=gain_raw[:], in_=strength.rearrange("(p c) -> p c", c=4))
+
+        nc.vector.memset(base_plane[:].bitcast(I32), 0)
+        nc.vector.memset(sal_plane[:].bitcast(I32), 0)
+        nc.vector.memset(table_in[:], 0.0)
+        nc.scalar.activation(out=table_out[:], in_=table_in[:], func=ACT.Abs)
+        make_identity(nc, ident[:])
+
+        lo, hi = range(2), range(2, PASSES)
+        load_half(0, 0)
+        load_gain()
+        load_sal_scales(nc.sync)
+        load_salience(0)
+        load_half(1, 0)
+        load_base_scales(nc.sync)
+        load_base(0)
+        load_half(2, 0)
+        load_half(0, 1)
+        load_salience(1)
+        load_half(1, 1)
+        load_base(1)
+        load_half(2, 1)
+        load_pair(3)
+        load_pair(4)
+        for g in range(PASSES):
+            load_tuned(g)
+        for i in range(5, TILES):
+            load_pair(i)
+
+        def flip(i, h):
+            turn(i, h, slot(i, h) % 2)
+            evacuate(i, h, slot(i, h) % 2)
+
+        def both(step, i):
+            step(i, 0)
+            step(i, 1)
+
+        units = [(i, h) for h in range(2) for i in range(SPLIT)]
+        subtract(0, 0)
+        flip(0, 0)
+        spread_gain(bank[7])
+        quantize_d(0, 0)
+        mul_v(0, lo)
+        for s, (i, h) in enumerate(units):
+            pp = hi if h else lo
+            if s + 1 < len(units):
+                subtract(*units[s + 1])
+                flip(*units[s + 1])
+                if s > 0:
+                    quantize_d(i, h)
+            else:
+                weigh(0)
+                quantize_d(i, h)
+                mul_v(i, pp)
+                both(subtract, 3)
+                both(flip, 3)
+            if 0 < s < len(units) - 1:
+                mul_v(i, pp)
+            if h:
+                take_abs(i)
+            mul_a(i, pp)
+        quantize_d(3, 0)
+        subtract(4, 0)
+        quantize_d(3, 1)
+        mul_v(3)
+        subtract(4, 1)
+        weigh(1)
+        mix_scalar(0)
+        both(flip, 4)
+        take_abs(3)
+        mul_a(3)
+        mix_vector(0)
+        mix_vector(1)
+        both(quantize_d, 4)
+        mul_a(4)
+        mul_v(4)
+        quantize_tuned(0)
+        mix_scalar(1)
+        mix_scalar(2)
+        mix_vector(2)
+        mix_vector(3)
+        quantize_tuned(1)
+        for g in range(2):
+            for j in range(5):
+                mul_r(j, g)
+        mix_scalar(3)
+        both(subtract, 5)
+        quantize_tuned(2)
+        both(flip, 5)
+        take_abs(4)
+        quantize_tuned(3)
+        weigh(2)
+        both(quantize_d, 5)
+        for j in range(5):
+            mul_r(j, 2)
+            mul_r(j, 3)
+        finish(0)
+        store(0)
+        both(subtract, 6)
+        for i in range(5, TILES):
+            mul_v(i)
+            if i + 1 < TILES:
+                both(flip, i + 1)
+            if i == 5:
+                finish(1)
+                store(1)
+                finish(2)
+                store(2)
+                weigh(3)
+            if i == 6:
+                weigh(4)
+                finish(4)
+                store(4)
+            if i + 1 < TILES:
+                both(quantize_d, i + 1)
+            if i > 5:
+                finish(i - 1)
+                store(i - 1)
+            take_abs(i)
+            mul_a(i)
+            if i + 2 < TILES:
+                both(subtract, i + 2)
+            if i == 5:
+                finish(3)
+                store(3)
+            weigh(i)
+            for g in range(4):
+                mul_r(i, g)
+        finish(7)
+        store(7)

@@ -17,15 +17,19 @@ ALU = mybir.AluOpType
 ACT = mybir.ActivationFunctionType
 
 P = 128
-PASSES = K // 512
+K_PASS = 4 * P
+PASSES = K // K_PASS
 TILES = M // P
 HALF = K // 2
-SPLIT = 3
-FACTORS = 8
-V_BANKS = [2, 3, 4, 2, 2, 2, 2, 2]
-AR_BANKS = [5, 6, 7, 3, 4, 5, 6, 7]
-VCOLS = 256
+SIDE_BY_SIDE = 3
+LOADED_IN_HALVES = 4
+BEFORE_TUNED = 5
+WEIGHED_EARLY = 2
 RING = 4
+V_BANK = [2, 3, 4] + [2] * (TILES - SIDE_BY_SIDE)
+SUM_BANK = [5, 6, 7, 3, 4, 5, 6, 7]
+VECTOR_COLUMNS = [384, 256, 256, 256]
+CATCH_UP = (2, 2)
 
 
 def tile_preference_attribute_margins_s10_kernel(
@@ -37,80 +41,96 @@ def tile_preference_attribute_margins_s10_kernel(
         ps = ctx.enter_context(tc.psum_pool(name="ps", bufs=1))
         ctx.enter_context(tc.manual_schedule())
 
-        def tiles(pool, stem, count, shape, dtype):
-            return [pool.tile(shape, dtype, name="%s%d" % (stem, j), align_bytes=64) for j in range(count)]
+        def tile(name, shape, dtype):
+            return sb.tile(shape, dtype, name=name, align_bytes=64)
+
+        def tiles(stem, count, shape, dtype):
+            return [tile("%s%d" % (stem, j), shape, dtype) for j in range(count)]
 
         bank = [ps.tile([P, N], F32, name="bank%d" % j) for j in range(8)]
-        turn_bank = bank[:2]
-        v_bank = [bank[j] for j in V_BANKS]
-        ar_bank = [bank[j] for j in AR_BANKS]
 
-        ident = sb.tile([P, P], F32, name="ident", align_bytes=64)
-        c_half = tiles(sb, "ch", 2 * SPLIT, [P, HALF], BF16)
-        r_half = tiles(sb, "rh", 2 * SPLIT, [P, HALF], BF16)
-        c_raw = tiles(sb, "c", TILES - SPLIT, [P, K], BF16)
-        r_raw = tiles(sb, "r", TILES - SPLIT, [P, K], BF16)
-        sal_codes = tiles(sb, "sc", 2, [P, 2, N], U32)
-        sal_plane = sb.tile([P, N], U8, name="sp", align_bytes=64)
-        base_codes = tiles(sb, "bc", 2, [P, 2, 2 * N], U8)
-        base_plane = sb.tile([P, PASSES, N], U8, name="bp", align_bytes=64)
-        tuned_raw = tiles(sb, "tr", PASSES, [P, 4, N], BF16)
-        tuned_mix = tiles(sb, "tm", PASSES, [P, 4 * N], BF16)
-        tuned_codes = tiles(sb, "tc", PASSES, [P, N], U32)
-        tuned_plane = tiles(sb, "tp", PASSES, [P, N], U8)
-        d_sorted = tiles(sb, "d", RING, [P, HALF], BF16)
-        d_turned = tiles(sb, "dt", RING, [P, HALF], BF16)
-        d_codes = tiles(sb, "dc", 2 * TILES, [P, 2 * P], U32)
-        d_plane = tiles(sb, "dp", 2 * TILES, [P, 2 * P], U8)
-        factor = tiles(sb, "w", FACTORS, [P, N], F32)
-        result = tiles(sb, "o", TILES, [P, N], F32)
-        gain_raw = sb.tile([P, 4], BF16, name="gr", align_bytes=64)
-        gain_col = sb.tile([P, 4], F32, name="gc", align_bytes=64)
-        gain = sb.tile([P, N], F32, name="gain", align_bytes=64)
-        table_in = sb.tile([P, 1], F32, name="ti", align_bytes=64)
-        table_out = sb.tile([P, 1], F32, name="to", align_bytes=64)
+        ident = tile("ident", [P, P], F32)
+        chosen_half = tiles("ch", 2 * LOADED_IN_HALVES, [P, HALF], BF16)
+        rejected_half = tiles("rh", 2 * LOADED_IN_HALVES, [P, HALF], BF16)
+        chosen_whole = tiles("c", TILES - LOADED_IN_HALVES, [P, K], BF16)
+        rejected_whole = tiles("r", TILES - LOADED_IN_HALVES, [P, K], BF16)
+        salience_codes = tiles("sc", 2, [P, 2, N], U32)
+        salience_plane = tile("sp", [P, N], U8)
+        base_codes = tiles("bc", 2, [P, 2, 2 * N], U8)
+        base_plane = tile("bp", [P, PASSES, N], U8)
+        tuned_raw = tiles("tr", PASSES, [P, 4, N], BF16)
+        tuned_grouped = tiles("tm", PASSES, [P, 4 * N], BF16)
+        tuned_codes = tiles("tc", PASSES, [P, N], U32)
+        tuned_plane = tiles("tp", PASSES, [P, N], U8)
+        d_sorted = tiles("d", RING, [P, HALF], BF16)
+        d_turned = tiles("dt", RING, [P, HALF], BF16)
+        d_codes = tiles("dc", 2 * TILES, [P, 2 * P], U32)
+        d_plane = tiles("dp", 2 * TILES, [P, 2 * P], U8)
+        factor = tiles("w", TILES, [P, N], F32)
+        result = tiles("o", TILES - 1, [P, N], F32)
+        last_result = tiles("last", 2, [P, N // 2], F32)
+        strength_raw = tile("gr", [P, 4], BF16)
+        strength_f32 = tile("gc", [P, 4], F32)
+        strength_rows = tile("gain", [P, N], F32)
+        preload_in = tile("ti", [P, 1], F32)
+        preload_out = tile("to", [P, 1], F32)
+
+        halves = [(i, h) for h in range(2) for i in range(SIDE_BY_SIDE)]
+        halves = halves + [(i, h) for i in range(SIDE_BY_SIDE, TILES) for h in range(2)]
 
         def slot(i, h):
-            return (h * SPLIT + i if i < SPLIT else 2 * i + h) % RING
+            return halves.index((i, h)) % RING
 
         def rows(i):
             return slice(i * P, (i + 1) * P)
 
-        def load_pair(i):
-            nc.sync.dma_start(out=c_raw[i - SPLIT][:], in_=chosen[rows(i), :])
-            nc.sync.dma_start(out=r_raw[i - SPLIT][:], in_=rejected[rows(i), :])
+        def k_half(h):
+            return slice(h * HALF, (h + 1) * HALF)
+
+        def passes_of(h):
+            return range(2 * h, 2 * h + 2)
+
 
         def load_half(i, h):
-            cols = slice(h * HALF, (h + 1) * HALF)
-            nc.sync.dma_start(out=c_half[2 * i + h][:], in_=chosen[rows(i), cols])
-            nc.sync.dma_start(out=r_half[2 * i + h][:], in_=rejected[rows(i), cols])
+            nc.sync.dma_start(out=chosen_half[2 * i + h][:], in_=chosen[rows(i), k_half(h)])
+            nc.sync.dma_start(out=rejected_half[2 * i + h][:], in_=rejected[rows(i), k_half(h)])
+
+        def load_whole(i):
+            nc.sync.dma_start(out=chosen_whole[i - LOADED_IN_HALVES][:], in_=chosen[rows(i), :])
+            nc.sync.dma_start(out=rejected_whole[i - LOADED_IN_HALVES][:], in_=rejected[rows(i), :])
 
         def load_salience(h):
-            src = salience_words[2 * h : 2 * h + 2].rearrange("g p n t -> p g (n t)").bitcast(I32)
-            nc.sync.dma_start(out=sal_codes[h][:].bitcast(I32), in_=src)
+            words = salience_words[2 * h : 2 * h + 2].rearrange("g p n t -> p g (n t)")
+            nc.sync.dma_start(out=salience_codes[h][:].bitcast(I32), in_=words.bitcast(I32))
 
         def load_base(h):
-            src = base_words[2 * h : 2 * h + 2].rearrange("g p b -> p g b").bitcast(I32)
-            nc.sync.dma_start(out=base_codes[h][:].bitcast(I32), in_=src)
+            words = base_words[2 * h : 2 * h + 2].rearrange("g p b -> p g b")
+            nc.sync.dma_start(out=base_codes[h][:].bitcast(I32), in_=words.bitcast(I32))
 
-        def load_sal_scales(eng):
-            for q in range(4):
-                src = salience_scales[:, 4 * q : 4 * q + 4, :].bitcast(I32)
-                eng.dma_start(out=sal_plane[32 * q : 32 * q + 16, :].bitcast(I32), in_=src)
+        def load_salience_scales():
+            for quadrant in range(4):
+                scale_rows = salience_scales[:, 4 * quadrant : 4 * quadrant + 4, :]
+                nc.sync.dma_start(
+                    out=salience_plane[32 * quadrant : 32 * quadrant + 16, :].bitcast(I32), in_=scale_rows.bitcast(I32)
+                )
 
-        def load_base_scales(eng):
-            for q in range(4):
-                src = base_scales[:, 4 * q : 4 * q + 4, :].rearrange("g r n -> r g n").bitcast(I32)
-                eng.dma_start(out=base_plane[32 * q : 32 * q + 4, :, :].bitcast(I32), in_=src)
+        def load_base_scales():
+            for quadrant in range(4):
+                scale_rows = base_scales[:, 4 * quadrant : 4 * quadrant + 4, :].rearrange("g r n -> r g n")
+                nc.sync.dma_start(
+                    out=base_plane[32 * quadrant : 32 * quadrant + 4, :, :].bitcast(I32), in_=scale_rows.bitcast(I32)
+                )
 
         def load_tuned(g):
-            src = tuned[g * 512 : (g + 1) * 512, :].rearrange("(p t) n -> p t n", t=4)
-            nc.sync.dma_start(out=tuned_raw[g][:], in_=src)
+            k_rows = tuned[g * K_PASS : (g + 1) * K_PASS, :].rearrange("(p t) n -> p t n", t=4)
+            nc.sync.dma_start(out=tuned_raw[g][:], in_=k_rows)
+
 
         def subtract(i, h):
-            cols = slice(h * HALF, (h + 1) * HALF)
-            a = c_half[2 * i + h][:] if i < SPLIT else c_raw[i - SPLIT][:, cols]
-            b = r_half[2 * i + h][:] if i < SPLIT else r_raw[i - SPLIT][:, cols]
+            if i < LOADED_IN_HALVES:
+                a, b = chosen_half[2 * i + h][:], rejected_half[2 * i + h][:]
+            else:
+                a, b = chosen_whole[i - LOADED_IN_HALVES][:, k_half(h)], rejected_whole[i - LOADED_IN_HALVES][:, k_half(h)]
             nc.vector.tensor_tensor(
                 out=d_sorted[slot(i, h)][:].rearrange("p (u w e) -> p u w e", u=2, e=2),
                 in0=a.rearrange("p (w u e) -> p u w e", u=2, e=2),
@@ -118,18 +138,16 @@ def tile_preference_attribute_margins_s10_kernel(
                 op=ALU.subtract,
             )
 
-        def turn(i, h, b):
+        def turn(i, h):
             words = d_sorted[slot(i, h)][:].bitcast(F32)
+            turned = bank[slot(i, h) % 2]
             for g in range(2):
                 for u in range(2):
-                    j = 2 * g + u
-                    s = u * 2 * P + g * P
-                    nc.tensor.transpose(turn_bank[b][:, j * P : (j + 1) * P], words[:, s : s + P], ident[:])
-
-        def evacuate(i, h, b):
+                    source = words[:, (2 * u + g) * P : (2 * u + g + 1) * P]
+                    nc.tensor.transpose(turned[:, (2 * g + u) * P : (2 * g + u + 1) * P], source, ident[:])
             nc.scalar.copy(
                 out=d_turned[slot(i, h)][:].bitcast(F32).rearrange("p (g m u) -> p g m u", g=2, u=2),
-                in_=turn_bank[b][:].rearrange("p (g u m) -> p g m u", g=2, u=2),
+                in_=turned[:].rearrange("p (g u m) -> p g m u", g=2, u=2),
             )
 
         def quantize_d(i, h):
@@ -137,190 +155,178 @@ def tile_preference_attribute_margins_s10_kernel(
                 out=d_codes[2 * i + h][:].bitcast(FP8X4), scales=d_plane[2 * i + h][:], in_=d_turned[slot(i, h)][:]
             )
 
-        def mx(bank, i, g, rhs, rhs_scale, start, stop):
-            cols = slice((g % 2) * P, (g % 2 + 1) * P)
+        def both_halves(step, i):
+            step(i, 0)
+            step(i, 1)
+
+
+        def group_tuned(g, copy, first, last):
+            copy(
+                out=tuned_grouped[g][:, 4 * first : 4 * last].rearrange("p (c i t) -> p c t i", i=4, t=4),
+                in_=tuned_raw[g][:, :, first:last].rearrange("p t (c i) -> p c t i", i=4),
+            )
+
+        def group_on_vector(g):
+            group_tuned(g, nc.vector.tensor_copy, 0, VECTOR_COLUMNS[g])
+
+        def group_on_scalar(g):
+            group_tuned(g, nc.scalar.copy, VECTOR_COLUMNS[g], N)
+
+        def quantize_tuned(g):
+            nc.vector.quantize_mx(out=tuned_codes[g][:].bitcast(FP8X4), scales=tuned_plane[g][:], in_=tuned_grouped[g][:])
+
+
+        def multiply(acc, i, g, codes, plane, start, stop):
+            tile_rows = slice((g % 2) * P, (g % 2 + 1) * P)
             nc.tensor.matmul_mx(
-                out=bank[:],
-                lhsT=d_codes[2 * i + g // 2][:, cols].bitcast(FP8X4),
-                lhsT_scale=d_plane[2 * i + g // 2][:, cols],
-                rhs=rhs,
-                rhs_scale=rhs_scale,
+                out=acc[:],
+                lhsT=d_codes[2 * i + g // 2][:, tile_rows].bitcast(FP8X4),
+                lhsT_scale=d_plane[2 * i + g // 2][:, tile_rows],
+                rhs=codes,
+                rhs_scale=plane,
                 start=start,
                 stop=stop,
             )
 
-        def mul_v(i, passes=range(PASSES)):
+        def times_salience(i, passes):
             for g in passes:
-                mx(v_bank[i], i, g, sal_codes[g // 2][:, g % 2, :].bitcast(FP8X4), sal_plane[4 * g :, :], g == 0, g == PASSES - 1)
+                codes = salience_codes[g // 2][:, g % 2, :].bitcast(FP8X4)
+                multiply(bank[V_BANK[i]], i, g, codes, salience_plane[4 * g :, :], g == 0, g == PASSES - 1)
 
-        def mul_a(i, passes=range(PASSES)):
+        def times_base(i, passes):
             for g in passes:
-                mx(ar_bank[i], i, g, base_codes[g // 2][:, g % 2, :].bitcast(FP4X4), base_plane[:, g, :], g == 0, False)
+                codes = base_codes[g // 2][:, g % 2, :].bitcast(FP4X4)
+                multiply(bank[SUM_BANK[i]], i, g, codes, base_plane[:, g, :], g == 0, False)
 
-        def mul_r(i, g):
-            mx(ar_bank[i], i, g, tuned_codes[g][:].bitcast(FP8X4), tuned_plane[g][:], False, g == PASSES - 1)
+        def times_tuned(i, g):
+            multiply(bank[SUM_BANK[i]], i, g, tuned_codes[g][:].bitcast(FP8X4), tuned_plane[g][:], False, g == PASSES - 1)
 
-        def mix(copy, g, c0, c1):
-            copy(
-                out=tuned_mix[g][:, 4 * c0 : 4 * c1].rearrange("p (c i t) -> p c t i", i=4, t=4),
-                in_=tuned_raw[g][:, :, c0:c1].rearrange("p t (c i) -> p c t i", i=4),
+
+        def spread_strength(scratch):
+            nc.vector.tensor_copy(out=strength_f32[:], in_=strength_raw[:])
+            for c in range(4):
+                column = strength_f32[:, c : c + 1].to_broadcast([P, P])
+                nc.tensor.transpose(scratch[:, c * P : (c + 1) * P], column, ident[:])
+            nc.scalar.copy(
+                out=strength_rows[:].rearrange("p (q c) -> p q c", c=4), in_=scratch[:].rearrange("p (c q) -> p q c", c=4)
             )
 
-        def mix_vector(g):
-            mix(nc.vector.tensor_copy, g, 0, VCOLS)
-
-        def mix_scalar(g):
-            mix(nc.scalar.copy, g, VCOLS, N)
-
-        def quantize_tuned(g):
-            nc.vector.quantize_mx(out=tuned_codes[g][:].bitcast(FP8X4), scales=tuned_plane[g][:], in_=tuned_mix[g][:])
-
         def take_abs(i):
-            nc.scalar.activation(out=factor[i % FACTORS][:], in_=v_bank[i][:], func=ACT.Abs)
+            nc.scalar.activation(out=factor[i][:], in_=bank[V_BANK[i]][:], func=ACT.Abs)
 
         def weigh(i):
-            nc.vector.tensor_tensor(out=factor[i % FACTORS][:], in0=factor[i % FACTORS][:], in1=gain[:], op=ALU.mult)
+            nc.vector.tensor_tensor(out=factor[i][:], in0=factor[i][:], in1=strength_rows[:], op=ALU.mult)
 
         def finish(i):
-            nc.vector.tensor_tensor(out=result[i][:], in0=ar_bank[i][:], in1=factor[i % FACTORS][:], op=ALU.mult)
-
-        def store(i):
+            nc.vector.tensor_tensor(out=result[i][:], in0=bank[SUM_BANK[i]][:], in1=factor[i][:], op=ALU.mult)
             nc.sync.dma_start(out=out[rows(i), :], in_=result[i][:])
 
-        def spread_gain(b):
-            nc.vector.tensor_copy(out=gain_col[:], in_=gain_raw[:])
-            for c in range(4):
-                nc.tensor.transpose(b[:, c * P : (c + 1) * P], gain_col[:, c : c + 1].to_broadcast([P, P]), ident[:])
-            nc.scalar.copy(out=gain[:].rearrange("p (q c) -> p q c", c=4), in_=b[:].rearrange("p (c q) -> p q c", c=4))
-
-        def load_gain():
-            nc.sync.dma_start(out=gain_raw[:], in_=strength.rearrange("(p c) -> p c", c=4))
+        def finish_last():
+            i = TILES - 1
+            for c in range(2):
+                cols = slice(c * N // 2, (c + 1) * N // 2)
+                nc.vector.tensor_tensor(out=last_result[c][:], in0=bank[SUM_BANK[i]][:, cols], in1=factor[i][:, cols], op=ALU.mult)
+                nc.sync.dma_start(out=out[rows(i), cols], in_=last_result[c][:])
 
         nc.vector.memset(base_plane[:].bitcast(I32), 0)
-        nc.vector.memset(sal_plane[:].bitcast(I32), 0)
-        nc.vector.memset(table_in[:], 0.0)
-        nc.scalar.activation(out=table_out[:], in_=table_in[:], func=ACT.Abs)
+        nc.vector.memset(salience_plane[:].bitcast(I32), 0)
+        nc.vector.memset(preload_in[:], 0.0)
+        nc.scalar.activation(out=preload_out[:], in_=preload_in[:], func=ACT.Abs)
         make_identity(nc, ident[:])
 
-        lo, hi = range(2), range(2, PASSES)
-        load_half(0, 0)
-        load_gain()
-        load_sal_scales(nc.sync)
-        load_salience(0)
-        load_half(1, 0)
-        load_base_scales(nc.sync)
-        load_base(0)
-        load_half(2, 0)
-        load_half(0, 1)
-        load_salience(1)
-        load_half(1, 1)
-        load_base(1)
-        load_half(2, 1)
-        load_pair(3)
-        load_pair(4)
+        for h in range(2):
+            load_half(0, h)
+            if h == 0:
+                nc.sync.dma_start(out=strength_raw[:], in_=strength.rearrange("(q c) -> q c", c=4))
+                load_salience_scales()
+            load_salience(h)
+            load_half(1, h)
+            if h == 0:
+                load_base_scales()
+            load_base(h)
+            load_half(2, h)
+        both_halves(load_half, SIDE_BY_SIDE)
+        load_whole(BEFORE_TUNED - 1)
         for g in range(PASSES):
             load_tuned(g)
-        for i in range(5, TILES):
-            load_pair(i)
+        for i in range(BEFORE_TUNED, TILES):
+            load_whole(i)
 
-        def flip(i, h):
-            turn(i, h, slot(i, h) % 2)
-            evacuate(i, h, slot(i, h) % 2)
-
-        def both(step, i):
-            step(i, 0)
-            step(i, 1)
-
-        units = [(i, h) for h in range(2) for i in range(SPLIT)]
         subtract(0, 0)
-        flip(0, 0)
-        spread_gain(bank[7])
+        turn(0, 0)
+        spread_strength(bank[SUM_BANK[SIDE_BY_SIDE - 1]])
         quantize_d(0, 0)
-        mul_v(0, lo)
-        for s, (i, h) in enumerate(units):
-            pp = hi if h else lo
-            if s + 1 < len(units):
-                subtract(*units[s + 1])
-                flip(*units[s + 1])
-                if s > 0:
-                    quantize_d(i, h)
+        times_salience(0, passes_of(0))
+        in_halves = halves[: 2 * LOADED_IN_HALVES]
+        for step, (i, h) in enumerate(in_halves):
+            if step + 1 < len(in_halves):
+                subtract(*in_halves[step + 1])
+                turn(*in_halves[step + 1])
             else:
-                weigh(0)
+                both_halves(subtract, LOADED_IN_HALVES)
+                both_halves(turn, LOADED_IN_HALVES)
+            if step > 0:
                 quantize_d(i, h)
-                mul_v(i, pp)
-                both(subtract, 3)
-                both(flip, 3)
-            if 0 < s < len(units) - 1:
-                mul_v(i, pp)
-            if h:
+                before, before_half = in_halves[step - 1]
+                if before_half == 1 and before < WEIGHED_EARLY:
+                    weigh(before)
+                times_salience(i, passes_of(h))
+            if h == 1:
                 take_abs(i)
-            mul_a(i, pp)
-        quantize_d(3, 0)
-        subtract(4, 0)
-        quantize_d(3, 1)
-        mul_v(3)
-        subtract(4, 1)
-        weigh(1)
-        mix_scalar(0)
-        both(flip, 4)
-        take_abs(3)
-        mul_a(3)
-        mix_vector(0)
-        mix_vector(1)
-        both(quantize_d, 4)
-        mul_a(4)
-        mul_v(4)
-        quantize_tuned(0)
-        mix_scalar(1)
-        mix_scalar(2)
-        mix_vector(2)
-        mix_vector(3)
-        quantize_tuned(1)
-        for g in range(2):
-            for j in range(5):
-                mul_r(j, g)
-        mix_scalar(3)
-        both(subtract, 5)
-        quantize_tuned(2)
-        both(flip, 5)
-        take_abs(4)
-        quantize_tuned(3)
-        weigh(2)
-        both(quantize_d, 5)
-        for j in range(5):
-            mul_r(j, 2)
-            mul_r(j, 3)
-        finish(0)
-        store(0)
-        both(subtract, 6)
-        for i in range(5, TILES):
-            mul_v(i)
+            times_base(i, passes_of(h))
+
+        i = BEFORE_TUNED - 1
+        group_on_vector(0)
+        group_on_scalar(0)
+        both_halves(quantize_d, i)
+        times_base(i, range(PASSES))
+        times_salience(i, range(PASSES))
+        for g in range(1, PASSES):
+            group_on_vector(g)
+            group_on_scalar(g)
+            if g == PASSES - 1:
+                both_halves(subtract, BEFORE_TUNED)
+            quantize_tuned(g - 1)
+
+        for g in passes_of(0):
+            for j in range(BEFORE_TUNED):
+                times_tuned(j, g)
+        both_halves(turn, BEFORE_TUNED)
+        take_abs(i)
+        quantize_tuned(PASSES - 1)
+        both_halves(quantize_d, BEFORE_TUNED)
+        for g in passes_of(1):
+            for j in range(BEFORE_TUNED):
+                times_tuned(j, g)
+
+        due = []
+        for j in range(BEFORE_TUNED):
+            due.extend([(weigh, j), (finish, j)] if j >= WEIGHED_EARLY else [(finish, j)])
+
+        def catch_up(count):
+            for step, j in due[:count]:
+                step(j)
+                due.remove((step, j))
+
+        catch_up(1)
+        both_halves(subtract, BEFORE_TUNED + 1)
+
+        for i in range(BEFORE_TUNED, TILES):
+            times_salience(i, range(PASSES))
             if i + 1 < TILES:
-                both(flip, i + 1)
-            if i == 5:
-                finish(1)
-                store(1)
-                finish(2)
-                store(2)
-                weigh(3)
-            if i == 6:
-                weigh(4)
-                finish(4)
-                store(4)
+                both_halves(turn, i + 1)
+            catch_up(CATCH_UP[0])
             if i + 1 < TILES:
-                both(quantize_d, i + 1)
-            if i > 5:
-                finish(i - 1)
-                store(i - 1)
+                both_halves(quantize_d, i + 1)
             take_abs(i)
-            mul_a(i)
+            times_base(i, range(PASSES))
             if i + 2 < TILES:
-                both(subtract, i + 2)
-            if i == 5:
-                finish(3)
-                store(3)
-            weigh(i)
-            for g in range(4):
-                mul_r(i, g)
-        finish(7)
-        store(7)
+                both_halves(subtract, i + 2)
+            due.append((weigh, i))
+            catch_up(CATCH_UP[1])
+            for g in range(PASSES):
+                times_tuned(i, g)
+            if i + 1 < TILES:
+                due.append((finish, i))
+        assert not due
+        finish_last()

@@ -28,7 +28,7 @@ WEIGHED_EARLY = 2
 RING = 4
 V_BANK = [2, 3, 4] + [2] * (TILES - SIDE_BY_SIDE)
 SUM_BANK = [5, 6, 7, 3, 4, 5, 6, 7]
-VECTOR_COLUMNS = [384, 256, 256, 256]
+VECTOR_COLUMNS = [384, 256, 256, 128]
 CATCH_UP = (2, 2)
 
 
@@ -301,14 +301,16 @@ def tile_preference_attribute_margins_s10_kernel(
 
         due = []
         for j in range(BEFORE_TUNED):
-            due.extend([(weigh, j), (finish, j)] if j >= WEIGHED_EARLY else [(finish, j)])
+            if j + WEIGHED_EARLY < BEFORE_TUNED:
+                due.append((weigh, j + WEIGHED_EARLY))
+            due.append((finish, j))
 
         def catch_up(count):
             for step, j in due[:count]:
                 step(j)
                 due.remove((step, j))
 
-        catch_up(1)
+        catch_up(2)
         both_halves(subtract, BEFORE_TUNED + 1)
 
         for i in range(BEFORE_TUNED, TILES):
@@ -318,15 +320,15 @@ def tile_preference_attribute_margins_s10_kernel(
             catch_up(CATCH_UP[0])
             if i + 1 < TILES:
                 both_halves(quantize_d, i + 1)
+            if i > BEFORE_TUNED:
+                finish(i - 1)
             take_abs(i)
             times_base(i, range(PASSES))
             if i + 2 < TILES:
                 both_halves(subtract, i + 2)
-            due.append((weigh, i))
             catch_up(CATCH_UP[1])
+            weigh(i)
             for g in range(PASSES):
                 times_tuned(i, g)
-            if i + 1 < TILES:
-                due.append((finish, i))
         assert not due
         finish_last()

@@ -22,14 +22,15 @@ PASSES = K // K_PASS
 TILES = M // P
 HALF = K // 2
 SIDE_BY_SIDE = 3
-LOADED_IN_HALVES = 4
+MULTIPLIED_IN_HALVES = 4
+LOADED_IN_HALVES = 5
 BEFORE_TUNED = 5
 WEIGHED_EARLY = 2
 RING = 4
 V_BANK = [2, 3, 4] + [2] * (TILES - SIDE_BY_SIDE)
 SUM_BANK = [5, 6, 7, 3, 4, 5, 6, 7]
-VECTOR_COLUMNS = [384, 256, 256, 128]
-CATCH_UP = (2, 2)
+VECTOR_COLUMNS = [384, 256, 384, 256]
+CATCH_UP = (2, 1)
 
 
 def tile_preference_attribute_margins_s10_kernel(
@@ -72,8 +73,6 @@ def tile_preference_attribute_margins_s10_kernel(
         strength_raw = tile("gr", [P, 4], BF16)
         strength_f32 = tile("gc", [P, 4], F32)
         strength_rows = tile("gain", [P, N], F32)
-        preload_in = tile("ti", [P, 1], F32)
-        preload_out = tile("to", [P, 1], F32)
 
         halves = [(i, h) for h in range(2) for i in range(SIDE_BY_SIDE)]
         halves = halves + [(i, h) for i in range(SIDE_BY_SIDE, TILES) for h in range(2)]
@@ -230,26 +229,29 @@ def tile_preference_attribute_margins_s10_kernel(
 
         nc.vector.memset(base_plane[:].bitcast(I32), 0)
         nc.vector.memset(salience_plane[:].bitcast(I32), 0)
-        nc.vector.memset(preload_in[:], 0.0)
-        nc.scalar.activation(out=preload_out[:], in_=preload_in[:], func=ACT.Abs)
         make_identity(nc, ident[:])
+        nc.scalar.activation(out=ident[:], in_=ident[:], func=ACT.Abs)
 
-        for h in range(2):
-            load_half(0, h)
-            if h == 0:
-                nc.sync.dma_start(out=strength_raw[:], in_=strength.rearrange("(q c) -> q c", c=4))
-                load_salience_scales()
-            load_salience(h)
-            load_half(1, h)
-            if h == 0:
-                load_base_scales()
-            load_base(h)
-            load_half(2, h)
-        both_halves(load_half, SIDE_BY_SIDE)
-        load_whole(BEFORE_TUNED - 1)
-        for g in range(PASSES):
+        load_half(0, 0)
+        nc.sync.dma_start(out=strength_raw[:], in_=strength.rearrange("(q c) -> q c", c=4))
+        load_salience_scales()
+        load_salience(0)
+        load_half(1, 0)
+        load_base_scales()
+        load_base(0)
+        load_half(2, 0)
+        load_half(0, 1)
+        load_half(1, 1)
+        load_salience(1)
+        load_half(2, 1)
+        load_base(1)
+        for i in range(SIDE_BY_SIDE, LOADED_IN_HALVES):
+            both_halves(load_half, i)
+        for g in range(PASSES - 1):
             load_tuned(g)
-        for i in range(BEFORE_TUNED, TILES):
+        load_whole(BEFORE_TUNED)
+        load_tuned(PASSES - 1)
+        for i in range(BEFORE_TUNED + 1, TILES):
             load_whole(i)
 
         subtract(0, 0)
@@ -257,14 +259,14 @@ def tile_preference_attribute_margins_s10_kernel(
         spread_strength(bank[SUM_BANK[SIDE_BY_SIDE - 1]])
         quantize_d(0, 0)
         times_salience(0, passes_of(0))
-        in_halves = halves[: 2 * LOADED_IN_HALVES]
+        in_halves = halves[: 2 * MULTIPLIED_IN_HALVES]
         for step, (i, h) in enumerate(in_halves):
             if step + 1 < len(in_halves):
                 subtract(*in_halves[step + 1])
                 turn(*in_halves[step + 1])
             else:
-                both_halves(subtract, LOADED_IN_HALVES)
-                both_halves(turn, LOADED_IN_HALVES)
+                both_halves(subtract, MULTIPLIED_IN_HALVES)
+                both_halves(turn, MULTIPLIED_IN_HALVES)
             if step > 0:
                 quantize_d(i, h)
                 before, before_half = in_halves[step - 1]
@@ -281,16 +283,18 @@ def tile_preference_attribute_margins_s10_kernel(
         both_halves(quantize_d, i)
         times_base(i, range(PASSES))
         times_salience(i, range(PASSES))
-        for g in range(1, PASSES):
+        for g in range(1, PASSES - 1):
             group_on_vector(g)
             group_on_scalar(g)
-            if g == PASSES - 1:
-                both_halves(subtract, BEFORE_TUNED)
             quantize_tuned(g - 1)
 
         for g in passes_of(0):
             for j in range(BEFORE_TUNED):
                 times_tuned(j, g)
+        quantize_tuned(PASSES - 2)
+        both_halves(subtract, BEFORE_TUNED)
+        group_on_vector(PASSES - 1)
+        group_on_scalar(PASSES - 1)
         both_halves(turn, BEFORE_TUNED)
         take_abs(i)
         quantize_tuned(PASSES - 1)
@@ -310,8 +314,8 @@ def tile_preference_attribute_margins_s10_kernel(
                 step(j)
                 due.remove((step, j))
 
-        catch_up(2)
         both_halves(subtract, BEFORE_TUNED + 1)
+        catch_up(2)
 
         for i in range(BEFORE_TUNED, TILES):
             times_salience(i, range(PASSES))

from contextlib import ExitStack

import concourse.mybir as mybir
from concourse.masks import make_identity

M, K, N = 1024, 2048, 512
FLOPS = 3 * 2 * M * K * N

F32 = mybir.dt.float32
BF16 = mybir.dt.bfloat16
U32 = mybir.dt.uint32
I32 = mybir.dt.int32
U8 = mybir.dt.uint8
FP8X4 = mybir.dt.float8_e4m3fn_x4
FP4X4 = mybir.dt.float4_e2m1fn_x4
ALU = mybir.AluOpType
ACT = mybir.ActivationFunctionType

P = 128
K_PASS = 4 * P
PASSES = K // K_PASS
TILES = M // P
HALF = K // 2
SIDE_BY_SIDE = 3
MULTIPLIED_IN_HALVES = 4
LOADED_IN_HALVES = 5
BEFORE_TUNED = 5
WEIGHED_EARLY = 2
RING = 4
V_BANK = [2, 3, 4] + [2] * (TILES - SIDE_BY_SIDE)
SUM_BANK = [5, 6, 7, 3, 4, 5, 6, 7]
VECTOR_COLUMNS = [384, 256, 384, 256]
CATCH_UP = (2, 1)


def tile_preference_attribute_margins_s10_kernel(
    tc, chosen, rejected, base_words, base_scales, salience_words, salience_scales, tuned, strength, out
):
    nc = tc.nc
    with ExitStack() as ctx:
        sb = ctx.enter_context(tc.tile_pool(name="sb", bufs=1))
        ps = ctx.enter_context(tc.psum_pool(name="ps", bufs=1))
        ctx.enter_context(tc.manual_schedule())

        def tile(name, shape, dtype):
            return sb.tile(shape, dtype, name=name, align_bytes=64)

        def tiles(stem, count, shape, dtype):
            return [tile("%s%d" % (stem, j), shape, dtype) for j in range(count)]

        bank = [ps.tile([P, N], F32, name="bank%d" % j) for j in range(8)]

        ident = tile("ident", [P, P], F32)
        chosen_half = tiles("ch", 2 * LOADED_IN_HALVES, [P, HALF], BF16)
        rejected_half = tiles("rh", 2 * LOADED_IN_HALVES, [P, HALF], BF16)
        chosen_whole = tiles("c", TILES - LOADED_IN_HALVES, [P, K], BF16)
        rejected_whole = tiles("r", TILES - LOADED_IN_HALVES, [P, K], BF16)
        salience_codes = tiles("sc", 2, [P, 2, N], U32)
        salience_plane = tile("sp", [P, N], U8)
        base_codes = tiles("bc", 2, [P, 2, 2 * N], U8)
        base_plane = tile("bp", [P, PASSES, N], U8)
        tuned_raw = tiles("tr", PASSES, [P, 4, N], BF16)
        tuned_grouped = tiles("tm", PASSES, [P, 4 * N], BF16)
        tuned_codes = tiles("tc", PASSES, [P, N], U32)
        tuned_plane = tiles("tp", PASSES, [P, N], U8)
        d_sorted = tiles("d", RING, [P, HALF], BF16)
        d_turned = tiles("dt", RING, [P, HALF], BF16)
        d_codes = tiles("dc", 2 * TILES, [P, 2 * P], U32)
        d_plane = tiles("dp", 2 * TILES, [P, 2 * P], U8)
        factor = tiles("w", TILES, [P, N], F32)
        result = tiles("o", TILES - 1, [P, N], F32)
        last_result = tiles("last", 2, [P, N // 2], F32)
        strength_raw = tile("gr", [P, 4], BF16)
        strength_f32 = tile("gc", [P, 4], F32)
        strength_rows = tile("gain", [P, N], F32)

        halves = [(i, h) for h in range(2) for i in range(SIDE_BY_SIDE)]
        halves = halves + [(i, h) for i in range(SIDE_BY_SIDE, TILES) for h in range(2)]

        def slot(i, h):
            return halves.index((i, h)) % RING

        def rows(i):
            return slice(i * P, (i + 1) * P)

        def k_half(h):
            return slice(h * HALF, (h + 1) * HALF)

        def passes_of(h):
            return range(2 * h, 2 * h + 2)


        def load_half(i, h):
            nc.sync.dma_start(out=chosen_half[2 * i + h][:], in_=chosen[rows(i), k_half(h)])
            nc.sync.dma_start(out=rejected_half[2 * i + h][:], in_=rejected[rows(i), k_half(h)])

        def load_whole(i):
            nc.sync.dma_start(out=chosen_whole[i - LOADED_IN_HALVES][:], in_=chosen[rows(i), :])
            nc.sync.dma_start(out=rejected_whole[i - LOADED_IN_HALVES][:], in_=rejected[rows(i), :])

        def load_salience(h):
            words = salience_words[2 * h : 2 * h + 2].rearrange("g p n t -> p g (n t)")
            nc.sync.dma_start(out=salience_codes[h][:].bitcast(I32), in_=words.bitcast(I32))

        def load_base(h):
            words = base_words[2 * h : 2 * h + 2].rearrange("g p b -> p g b")
            nc.sync.dma_start(out=base_codes[h][:].bitcast(I32), in_=words.bitcast(I32))

        def load_salience_scales():
            for quadrant in range(4):
                scale_rows = salience_scales[:, 4 * quadrant : 4 * quadrant + 4, :]
                nc.sync.dma_start(
                    out=salience_plane[32 * quadrant : 32 * quadrant + 16, :].bitcast(I32), in_=scale_rows.bitcast(I32)
                )

        def load_base_scales():
            for quadrant in range(4):
                scale_rows = base_scales[:, 4 * quadrant : 4 * quadrant + 4, :].rearrange("g r n -> r g n")
                nc.sync.dma_start(
                    out=base_plane[32 * quadrant : 32 * quadrant + 4, :, :].bitcast(I32), in_=scale_rows.bitcast(I32)
                )

        def load_tuned(g):
            k_rows = tuned[g * K_PASS : (g + 1) * K_PASS, :].rearrange("(p t) n -> p t n", t=4)
            nc.sync.dma_start(out=tuned_raw[g][:], in_=k_rows)


        def subtract(i, h):
            if i < LOADED_IN_HALVES:
                a, b = chosen_half[2 * i + h][:], rejected_half[2 * i + h][:]
            else:
                a, b = chosen_whole[i - LOADED_IN_HALVES][:, k_half(h)], rejected_whole[i - LOADED_IN_HALVES][:, k_half(h)]
            nc.vector.tensor_tensor(
                out=d_sorted[slot(i, h)][:].rearrange("p (u w e) -> p u w e", u=2, e=2),
                in0=a.rearrange("p (w u e) -> p u w e", u=2, e=2),
                in1=b.rearrange("p (w u e) -> p u w e", u=2, e=2),
                op=ALU.subtract,
            )

        def turn(i, h):
            words = d_sorted[slot(i, h)][:].bitcast(F32)
            turned = bank[slot(i, h) % 2]
            for g in range(2):
                for u in range(2):
                    source = words[:, (2 * u + g) * P : (2 * u + g + 1) * P]
                    nc.tensor.transpose(turned[:, (2 * g + u) * P : (2 * g + u + 1) * P], source, ident[:])
            nc.scalar.copy(
                out=d_turned[slot(i, h)][:].bitcast(F32).rearrange("p (g m u) -> p g m u", g=2, u=2),
                in_=turned[:].rearrange("p (g u m) -> p g m u", g=2, u=2),
            )

        def quantize_d(i, h):
            nc.vector.quantize_mx(
                out=d_codes[2 * i + h][:].bitcast(FP8X4), scales=d_plane[2 * i + h][:], in_=d_turned[slot(i, h)][:]
            )

        def both_halves(step, i):
            step(i, 0)
            step(i, 1)


        def group_tuned(g, copy, first, last):
            copy(
                out=tuned_grouped[g][:, 4 * first : 4 * last].rearrange("p (c i t) -> p c t i", i=4, t=4),
                in_=tuned_raw[g][:, :, first:last].rearrange("p t (c i) -> p c t i", i=4),
            )

        def group_on_vector(g):
            group_tuned(g, nc.vector.tensor_copy, 0, VECTOR_COLUMNS[g])

        def group_on_scalar(g):
            group_tuned(g, nc.scalar.copy, VECTOR_COLUMNS[g], N)

        def quantize_tuned(g):
            nc.vector.quantize_mx(out=tuned_codes[g][:].bitcast(FP8X4), scales=tuned_plane[g][:], in_=tuned_grouped[g][:])


        def multiply(acc, i, g, codes, plane, start, stop):
            tile_rows = slice((g % 2) * P, (g % 2 + 1) * P)
            nc.tensor.matmul_mx(
                out=acc[:],
                lhsT=d_codes[2 * i + g // 2][:, tile_rows].bitcast(FP8X4),
                lhsT_scale=d_plane[2 * i + g // 2][:, tile_rows],
                rhs=codes,
                rhs_scale=plane,
                start=start,
                stop=stop,
            )

        def times_salience(i, passes):
            for g in passes:
                codes = salience_codes[g // 2][:, g % 2, :].bitcast(FP8X4)
                multiply(bank[V_BANK[i]], i, g, codes, salience_plane[4 * g :, :], g == 0, g == PASSES - 1)

        def times_base(i, passes):
            for g in passes:
                codes = base_codes[g // 2][:, g % 2, :].bitcast(FP4X4)
                multiply(bank[SUM_BANK[i]], i, g, codes, base_plane[:, g, :], g == 0, False)

        def times_tuned(i, g):
            multiply(bank[SUM_BANK[i]], i, g, tuned_codes[g][:].bitcast(FP8X4), tuned_plane[g][:], False, g == PASSES - 1)


        def spread_strength(scratch):
            nc.vector.tensor_copy(out=strength_f32[:], in_=strength_raw[:])
            for c in range(4):
                column = strength_f32[:, c : c + 1].to_broadcast([P, P])
                nc.tensor.transpose(scratch[:, c * P : (c + 1) * P], column, ident[:])
            nc.scalar.copy(
                out=strength_rows[:].rearrange("p (q c) -> p q c", c=4), in_=scratch[:].rearrange("p (c q) -> p q c", c=4)
            )

        def take_abs(i):
            nc.scalar.activation(out=factor[i][:], in_=bank[V_BANK[i]][:], func=ACT.Abs)

        def weigh(i):
            nc.vector.tensor_tensor(out=factor[i][:], in0=factor[i][:], in1=strength_rows[:], op=ALU.mult)

        def finish(i):
            nc.vector.tensor_tensor(out=result[i][:], in0=bank[SUM_BANK[i]][:], in1=factor[i][:], op=ALU.mult)
            nc.sync.dma_start(out=out[rows(i), :], in_=result[i][:])

        def finish_last():
            i = TILES - 1
            for c in range(2):
                cols = slice(c * N // 2, (c + 1) * N // 2)
                nc.vector.tensor_tensor(out=last_result[c][:], in0=bank[SUM_BANK[i]][:, cols], in1=factor[i][:, cols], op=ALU.mult)
                nc.sync.dma_start(out=out[rows(i), cols], in_=last_result[c][:])

        nc.vector.memset(base_plane[:].bitcast(I32), 0)
        nc.vector.memset(salience_plane[:].bitcast(I32), 0)
        make_identity(nc, ident[:])
        nc.scalar.activation(out=ident[:], in_=ident[:], func=ACT.Abs)

        load_half(0, 0)
        nc.sync.dma_start(out=strength_raw[:], in_=strength.rearrange("(q c) -> q c", c=4))
        load_salience_scales()
        load_salience(0)
        load_half(1, 0)
        load_base_scales()
        load_base(0)
        load_half(2, 0)
        load_half(0, 1)
        load_half(1, 1)
        load_salience(1)
        load_half(2, 1)
        load_base(1)
        for i in range(SIDE_BY_SIDE, LOADED_IN_HALVES):
            both_halves(load_half, i)
        for g in range(PASSES - 1):
            load_tuned(g)
        load_whole(BEFORE_TUNED)
        load_tuned(PASSES - 1)
        for i in range(BEFORE_TUNED + 1, TILES):
            load_whole(i)

        subtract(0, 0)
        turn(0, 0)
        spread_strength(bank[SUM_BANK[SIDE_BY_SIDE - 1]])
        quantize_d(0, 0)
        times_salience(0, passes_of(0))
        in_halves = halves[: 2 * MULTIPLIED_IN_HALVES]
        for step, (i, h) in enumerate(in_halves):
            if step + 1 < len(in_halves):
                subtract(*in_halves[step + 1])
                turn(*in_halves[step + 1])
            else:
                both_halves(subtract, MULTIPLIED_IN_HALVES)
                both_halves(turn, MULTIPLIED_IN_HALVES)
            if step > 0:
                quantize_d(i, h)
                before, before_half = in_halves[step - 1]
                if before_half == 1 and before < WEIGHED_EARLY:
                    weigh(before)
                times_salience(i, passes_of(h))
            if h == 1:
                take_abs(i)
            times_base(i, passes_of(h))

        i = BEFORE_TUNED - 1
        group_on_vector(0)
        group_on_scalar(0)
        both_halves(quantize_d, i)
        times_base(i, range(PASSES))
        times_salience(i, range(PASSES))
        for g in range(1, PASSES - 1):
            group_on_vector(g)
            group_on_scalar(g)
            quantize_tuned(g - 1)

        for g in passes_of(0):
            for j in range(BEFORE_TUNED):
                times_tuned(j, g)
        quantize_tuned(PASSES - 2)
        both_halves(subtract, BEFORE_TUNED)
        group_on_vector(PASSES - 1)
        group_on_scalar(PASSES - 1)
        both_halves(turn, BEFORE_TUNED)
        take_abs(i)
        quantize_tuned(PASSES - 1)
        both_halves(quantize_d, BEFORE_TUNED)
        for g in passes_of(1):
            for j in range(BEFORE_TUNED):
                times_tuned(j, g)

        due = []
        for j in range(BEFORE_TUNED):
            if j + WEIGHED_EARLY < BEFORE_TUNED:
                due.append((weigh, j + WEIGHED_EARLY))
            due.append((finish, j))

        def catch_up(count):
            for step, j in due[:count]:
                step(j)
                due.remove((step, j))

        both_halves(subtract, BEFORE_TUNED + 1)
        catch_up(2)

        for i in range(BEFORE_TUNED, TILES):
            times_salience(i, range(PASSES))
            if i + 1 < TILES:
                both_halves(turn, i + 1)
            catch_up(CATCH_UP[0])
            if i + 1 < TILES:
                both_halves(quantize_d, i + 1)
            if i > BEFORE_TUNED:
                finish(i - 1)
            take_abs(i)
            times_base(i, range(PASSES))
            if i + 2 < TILES:
                both_halves(subtract, i + 2)
            catch_up(CATCH_UP[1])
            weigh(i)
            for g in range(PASSES):
                times_tuned(i, g)
        assert not due
        finish_last()
